import numpy as np
import ml_dtypes


def mxq(x, axis, fmt="e4m3"):
    dtype, down = {"e4m3": (ml_dtypes.float8_e4m3fn, 7), "e5m2": (ml_dtypes.float8_e5m2, 14)}[fmt]
    v = np.moveaxis(np.asarray(x, np.float32).astype(ml_dtypes.bfloat16).astype(np.float64), axis, -1)
    blocks = v.reshape(v.shape[:-1] + (-1, 32))
    amax = np.abs(blocks).max(-1, keepdims=True)
    byte = np.maximum(np.where(amax > 0, np.frexp(amax)[1] - 1 + 127, 0) - down, 1)
    scale = np.exp2(byte - 127.0)
    codes = (blocks / scale).astype(np.float32).astype(dtype).astype(np.float64)
    return np.moveaxis((codes * scale).reshape(v.shape), -1, axis)


WIDE = False


def mx_kscale(k):
    if not WIDE:
        return np.ones(k)
    levels = np.array([30, -30])
    if k % 512:
        return np.exp2(np.random.permutation(np.resize(levels, k // 32))).repeat(32)
    a = np.empty((k // 512, 16))
    for p in range(k // 512):
        a[p, :8] = np.random.permutation(np.resize(levels, 8))
        for g in range(8):
            far = levels[np.abs(levels - a[p, g]) >= 10]
            a[p, g + 8] = far[np.random.randint(len(far))]
    return np.exp2(a.ravel()).repeat(32)


BF16 = ml_dtypes.bfloat16


def bf(x):
    return np.asarray(x, np.float32).astype(BF16)


def f64(x):
    return np.asarray(x).astype(np.float64)


T, F, V, D = 2048, 2048, 1024, 512


def setup_inputs():
    s = mx_kscale(F)
    t = mx_kscale(V)
    logits = bf(2.0 * np.random.standard_normal((T, V)))
    lse = np.log(np.exp(f64(logits)).sum(axis=1))
    return {"frames": bf(np.random.standard_normal((T, D))),
            "hidden": bf(np.random.standard_normal((T, F)) * s),
            "w_out": bf(np.random.standard_normal((F, D)) / np.sqrt(F) / s[:, None]),
            "logits": logits,
            "lse": bf(lse),
            "gain": bf(V / 8.0 * (1.0 + 0.1 * np.random.standard_normal(V)) * t),
            "w_back": bf(np.random.standard_normal((V, D)) / np.sqrt(V) / t[:, None]),
            "bias": bf(0.3 * np.random.standard_normal(D))}


def reference(frames, hidden, w_out, logits, lse, gain, w_back, bias):
    post = np.exp(f64(logits) - f64(lse)[:, None]) * f64(gain)
    hq = mxq(f64(hidden), 1, "e4m3")
    wq = mxq(f64(w_out), 0, "e4m3")
    pq = mxq(post, 1, "e5m2")
    cq = mxq(f64(w_back), 0, "e4m3")
    y = (hq @ wq) + (pq @ cq)
    return y + f64(bias) + f64(frames)

@@ -1,0 +1,423 @@
+from contextlib import ExitStack
+
+import concourse.mybir as mybir
+from concourse.masks import make_identity
+
+T, F, V, D = 2048, 2048, 1024, 512
+FLOPS = 2 * T * (F + V) * D
+
+F32 = mybir.dt.float32
+BF16 = mybir.dt.bfloat16
+U32 = mybir.dt.uint32
+U8 = mybir.dt.uint8
+E4M3 = mybir.dt.float8_e4m3fn_x4
+E5M2 = mybir.dt.float8_e5m2_x4
+ADD = mybir.AluOpType.add
+MULT = mybir.AluOpType.mult
+EXP = mybir.ActivationFunctionType.Exp
+
+P = 128
+PACK = 4
+K_PASS = P * PACK
+TILES = T // P
+F_PASSES = F // K_PASS
+V_PASSES = V // K_PASS
+QBUFS = 4
+TBANKS = 4
+
+
+def tile_self_conditioned_ctc_s2_kernel(tc, frames, hidden, w_out, logits, lse, gain, w_back, bias, out):
+    nc = tc.nc
+    with ExitStack() as ctx:
+        keep = ctx.enter_context(tc.tile_pool(name="keep", bufs=1))
+        work = ctx.enter_context(tc.tile_pool(name="work", bufs=2))
+        psum = ctx.enter_context(tc.psum_pool(name="psum", bufs=1))
+        ctx.enter_context(tc.manual_schedule())
+
+        hidden_rows = hidden.rearrange("(p i) k -> p i k", i=TILES)
+        logit_rows = logits.rearrange("(p i) k -> p i k", i=TILES)
+        frame_rows = frames.rearrange("(p i) k -> p i k", i=TILES)
+        out_rows = out.rearrange("(p i) k -> p i k", i=TILES)
+
+        hid, logi, frm, w_raw, done, sorted_words, sorted_tile = {}, {}, {}, {}, {}, {}, {}
+        ex, post, hid_k, post_k, hid_q, post_q, w_k, w_q, acc, base = {}, {}, {}, {}, {}, {}, {}, {}, {}, {}
+
+        def load_rows(store, rows, label, first, count):
+            width = rows.shape[2]
+            t = keep.tile([P, count, width], BF16, name="%s%d" % (label, first), align_bytes=64)
+            nc.sync.dma_start(out=t[:], in_=rows[:, first : first + count, :])
+            for j in range(count):
+                store[first + j] = t[:, j, :]
+
+        def load_weight(g):
+            src = w_out[g * K_PASS : (g + 1) * K_PASS, :] if g < F_PASSES else w_back[(g - F_PASSES) * K_PASS : (g - F_PASSES + 1) * K_PASS, :]
+            t = keep.tile([P, PACK, D], BF16, name="w_raw", tag="w_raw%d" % g, align_bytes=64)
+            nc.sync.dma_start(out=t[:], in_=src.rearrange("(p j) n -> p j n", j=PACK))
+            w_raw[g] = t
+
+        def interleave_weight(g, engine, first=0, last=D):
+            if g not in w_k:
+                w_k[g] = work.tile([P, D, PACK], BF16, name="w_k", bufs=3, align_bytes=64)
+            dst = w_k[g][:, first:last, :].rearrange("p (c i) j -> p c j i", i=4)
+            src = w_raw[g][:, :, first:last].rearrange("p j (c i) -> p c j i", i=4)
+            if engine == "scalar":
+                nc.scalar.copy(out=dst, in_=src)
+            else:
+                nc.vector.tensor_copy(out=dst, in_=src)
+
+        def quantize_weight(g):
+            codes = keep.tile([P, D], U32, name="w_codes%d" % g, align_bytes=64)
+            scales = keep.tile([P, D], U8, name="w_scales%d" % g, align_bytes=64)
+            nc.vector.quantize_mx(out=codes[:].bitcast(E4M3), scales=scales[:], in_=w_k[g][:].rearrange("p n j -> p (n j)"))
+            w_q[g] = (codes, scales)
+
+        def transpose_bank():
+            return psum.tile([P, 2, 2, P], F32, name="turned", bufs=TBANKS)
+
+        def spread_gain():
+            words = gain_sb[:].rearrange("p g m -> p (g m)").bitcast(F32)
+            for u in range(2):
+                for g in range(2):
+                    col = 2 * g + u
+                    nc.tensor.transpose(gain_bank[:, u, g, :], words[:, col : col + 1].to_broadcast([P, P]), ident[:])
+
+        def spread_bias():
+            words = bias_sb[:].bitcast(F32)
+            bank = transpose_bank()
+            for a in range(2):
+                nc.tensor.transpose(bank[:, 0, a, :], words[:, a : a + 1].to_broadcast([P, P]), ident[:])
+            nc.scalar.copy(out=bias_all[:].bitcast(F32).rearrange("p (n a) -> p n a", a=2), in_=bank[:, 0, :, :].rearrange("p a n -> p n a"))
+
+        def exponentiate(i):
+            t = work.tile([P, V], F32, name="ex", bufs=2, align_bytes=64)
+            nc.scalar.activation(
+                out=t[:].rearrange("p (u c e) -> p u c e", u=2, e=2),
+                in_=logi[i].rearrange("p (c u e) -> p u c e", u=2, e=2),
+                func=EXP,
+                bias=neg_lse[:, i : i + 1],
+            )
+            ex[i] = t
+
+        def weigh(i):
+            t = work.tile([P, V], BF16, name="post", bufs=3, align_bytes=64)
+            nc.vector.tensor_tensor(out=t[:], in0=ex[i][:], in1=gain_bank[:].rearrange("p u g n -> p (u g n)").bitcast(BF16), op=MULT)
+            post[i] = t
+
+        def sort_hidden(i, first, count, engine):
+            if i not in sorted_tile:
+                sorted_tile[i] = work.tile([P, F_PASSES, 2, P], F32, name="sorted", tag="w_k", bufs=3, align_bytes=64)
+            words = hid[i].bitcast(F32)[:, first * 256 : (first + count) * 256].rearrange("p (g c u) -> p g u c", g=count, u=2)
+            if engine == "scalar":
+                nc.scalar.copy(out=sorted_tile[i][:, first : first + count, :, :], in_=words)
+            else:
+                nc.vector.tensor_copy(out=sorted_tile[i][:, first : first + count, :, :], in_=words)
+            for g in range(first, first + count):
+                sorted_words[i, g] = sorted_tile[i][:, g, :, :]
+
+        def turn_hidden(i, half):
+            words = hid[i].bitcast(F32)
+            bank = transpose_bank()
+            for g in range(2):
+                first = (2 * half + g) * 256
+                for u in range(2):
+                    if (i, 2 * half + g) in sorted_words:
+                        src = sorted_words[i, 2 * half + g][:, u, :]
+                    else:
+                        src = words[:, first + u : first + 256 : 2]
+                    nc.tensor.transpose(bank[:, g, u, :], src, ident[:])
+            if half == 0:
+                hid_k[i] = work.tile([P, F], BF16, name="hid_k", bufs=2, align_bytes=64)
+            dst = hid_k[i][:, half * 1024 : (half + 1) * 1024].bitcast(F32)
+            nc.scalar.copy(out=dst.rearrange("p (g r u) -> p g r u", g=2, u=2), in_=bank[:].rearrange("p g u r -> p g r u"))
+
+        def turn_post(i):
+            words = post[i][:].bitcast(F32)
+            bank = transpose_bank()
+            for g in range(2):
+                for u in range(2):
+                    first = u * 256 + g * P
+                    nc.tensor.transpose(bank[:, g, u, :], words[:, first : first + P], ident[:])
+            post_k[i] = keep.tile([P, V], BF16, name="post_k", tag="shared%d" % (i % 4), align_bytes=64)
+            dst = post_k[i][:].bitcast(F32)
+            nc.scalar.copy(out=dst.rearrange("p (g r u) -> p g r u", g=2, u=2), in_=bank[:].rearrange("p g u r -> p g r u"))
+
+        def quantize_hidden(i):
+            codes = work.tile([P, F // PACK], U32, name="hid_codes", bufs=QBUFS, align_bytes=64)
+            scales = work.tile([P, F // PACK], U8, name="hid_scales", bufs=QBUFS, align_bytes=64)
+            nc.vector.quantize_mx(out=codes[:].bitcast(E4M3), scales=scales[:], in_=hid_k[i][:])
+            hid_q[i] = (codes, scales)
+
+        def quantize_post(i):
+            codes = work.tile([P, V // PACK], U32, name="post_codes", bufs=QBUFS, align_bytes=64)
+            scales = work.tile([P, V // PACK], U8, name="post_scales", bufs=QBUFS, align_bytes=64)
+            nc.vector.quantize_mx(out=codes[:].bitcast(E5M2), scales=scales[:], in_=post_k[i][:])
+            post_q[i] = (codes, scales)
+
+        def multiply(i, passes):
+            for g in passes:
+                done[i] = done.get(i, 0) + 1
+                if done[i] == 1:
+                    acc[i] = psum.tile([P, D], F32, name="acc", bufs=7 - TBANKS)
+                if g < F_PASSES:
+                    (codes, scales), fmt, c = hid_q[i], E4M3, g
+                else:
+                    (codes, scales), fmt, c = post_q[i], E5M2, g - F_PASSES
+                nc.tensor.matmul_mx(
+                    out=acc[i][:],
+                    lhsT=codes[:, c * P : (c + 1) * P].bitcast(fmt),
+                    lhsT_scale=scales[:, c * P : (c + 1) * P],
+                    rhs=w_q[g][0][:].bitcast(E4M3),
+                    rhs_scale=w_q[g][1][:],
+                    start=(done[i] == 1),
+                    stop=(done[i] == F_PASSES + V_PASSES),
+                )
+
+        def add_bias(i, engine):
+            base[i] = keep.tile([P, D], F32, name="base", tag="shared%d" % (i % 4), align_bytes=64)
+            engine.tensor_tensor(out=base[i][:], in0=frm[i], in1=bias_all[:], op=ADD)
+
+        def finish(i, parts=1):
+            tag = "res%d" % i if i < TILES - 6 else "w_raw%d" % (i - TILES + 6)
+            res = keep.tile([P, D], F32, name="res", tag=tag, align_bytes=64)
+            width = D // parts
+            for c in range(0, D, width):
+                nc.vector.tensor_tensor(out=res[:, c : c + width], in0=acc[i][:, c : c + width], in1=base[i][:, c : c + width], op=ADD)
+                nc.sync.dma_start(out=out_rows[:, i, c : c + width], in_=res[:, c : c + width])
+
+        ident = keep.tile([P, P], F32, name="ident", align_bytes=64)
+        make_identity(nc, ident[:])
+
+        lse_sb = keep.tile([P, TILES], BF16, name="lse_sb")
+        gain_sb = keep.tile([P, 2, 4], BF16, name="gain_sb")
+        bias_sb = keep.tile([P, 4], BF16, name="bias_sb")
+        neg_lse = keep.tile([P, TILES], F32, name="neg_lse")
+        gain_bank = psum.tile([P, 2, 2, P], F32, name="gain_bank")
+        bias_all = keep.tile([P, D], BF16, name="bias_all", align_bytes=64)
+
+        nc.sync.dma_start(out=lse_sb[:], in_=lse.rearrange("(p i) -> p i", i=TILES))
+        nc.sync.dma_start(out=gain_sb[:], in_=gain.rearrange("(g p m) -> p g m", g=2, m=4))
+        load_rows(logi, logit_rows, "logi", 0, 1)
+        load_rows(hid, hidden_rows, "hid", 0, 1)
+        load_weight(0)
+        load_rows(logi, logit_rows, "logi", 1, 1)
+        load_weight(1)
+        load_rows(hid, hidden_rows, "hid", 1, 1)
+        load_rows(logi, logit_rows, "logi", 2, 1)
+        load_weight(2)
+        load_weight(3)
+        load_rows(hid, hidden_rows, "hid", 2, 1)
+        nc.sync.dma_start(out=bias_sb[:], in_=bias.rearrange("(p m) -> p m", m=4))
+        load_weight(4)
+        load_rows(logi, logit_rows, "logi", 3, 1)
+        load_weight(5)
+        load_rows(hid, hidden_rows, "hid", 3, 1)
+        load_rows(frm, frame_rows, "frm", 0, 4)
+        load_rows(logi, logit_rows, "logi", 4, 1)
+        load_rows(hid, hidden_rows, "hid", 4, 1)
+        load_rows(logi, logit_rows, "logi", 5, 1)
+        load_rows(hid, hidden_rows, "hid", 5, 1)
+        load_rows(frm, frame_rows, "frm", 4, 4)
+        load_rows(logi, logit_rows, "logi", 6, 2)
+        load_rows(hid, hidden_rows, "hid", 6, 2)
+        load_rows(logi, logit_rows, "logi", 8, 2)
+        load_rows(hid, hidden_rows, "hid", 8, 2)
+        load_rows(frm, frame_rows, "frm", 8, 4)
+        load_rows(logi, logit_rows, "logi", 10, 2)
+        load_rows(hid, hidden_rows, "hid", 10, 2)
+        load_rows(logi, logit_rows, "logi", 12, 2)
+        load_rows(hid, hidden_rows, "hid", 12, 2)
+        load_rows(frm, frame_rows, "frm", 12, 4)
+        load_rows(logi, logit_rows, "logi", 14, 2)
+        load_rows(hid, hidden_rows, "hid", 14, 2)
+        nc.vector.tensor_scalar(out=neg_lse[:], in0=lse_sb[:], scalar1=-1.0, scalar2=None, op0=MULT)
+        exponentiate(0)
+        spread_gain()
+        weigh(0)
+        turn_hidden(0, 0)
+        turn_hidden(0, 1)
+        exponentiate(1)
+        interleave_weight(0, "vector")
+        interleave_weight(1, "vector", 0, 256)
+        weigh(1)
+        turn_post(0)
+        interleave_weight(1, "scalar", 256, 512)
+        quantize_hidden(0)
+        quantize_weight(0)
+        quantize_post(0)
+        quantize_weight(1)
+        turn_hidden(1, 0)
+        turn_hidden(1, 1)
+        exponentiate(2)
+        interleave_weight(2, "vector")
+        interleave_weight(3, "vector", 0, 256)
+        weigh(2)
+        turn_post(1)
+        interleave_weight(3, "scalar", 256, 512)
+        multiply(0, [0, 1])
+        quantize_hidden(1)
+        quantize_weight(2)
+        quantize_post(1)
+        quantize_weight(3)
+        turn_hidden(2, 0)
+        turn_hidden(2, 1)
+        spread_bias()
+        exponentiate(3)
+        interleave_weight(4, "vector")
+        interleave_weight(5, "vector", 0, 256)
+        weigh(3)
+        turn_post(2)
+        interleave_weight(5, "scalar", 256, 512)
+        multiply(0, [2, 3])
+        multiply(1, [0, 1, 2, 3])
+        quantize_hidden(2)
+        quantize_weight(4)
+        quantize_post(2)
+        quantize_weight(5)
+        add_bias(0, nc.vector)
+        add_bias(1, nc.vector)
+        add_bias(2, nc.vector)
+        turn_hidden(3, 0)
+        turn_hidden(3, 1)
+        exponentiate(4)
+        weigh(4)
+        turn_post(3)
+        exponentiate(5)
+        multiply(0, [4, 5])
+        multiply(1, [4, 5])
+        multiply(2, [0, 1, 2, 3, 4, 5])
+        quantize_hidden(3)
+        quantize_post(3)
+        add_bias(3, nc.gpsimd)
+        turn_hidden(4, 0)
+        turn_hidden(4, 1)
+        finish(0)
+        weigh(5)
+        turn_post(4)
+        exponentiate(6)
+        multiply(3, [0, 1, 2, 3, 4, 5])
+        sort_hidden(5, 0, 3, "vector")
+        quantize_hidden(4)
+        quantize_post(4)
+        add_bias(4, nc.gpsimd)
+        finish(1)
+        finish(2)
+        turn_hidden(5, 0)
+        turn_hidden(5, 1)
+        finish(3)
+        weigh(6)
+        turn_post(5)
+        exponentiate(7)
+        multiply(4, [0, 1, 2, 3, 4, 5])
+        sort_hidden(6, 0, 3, "vector")
+        quantize_hidden(5)
+        quantize_post(5)
+        add_bias(5, nc.gpsimd)
+        turn_hidden(6, 0)
+        turn_hidden(6, 1)
+        finish(4)
+        weigh(7)
+        turn_post(6)
+        exponentiate(8)
+        multiply(5, [0, 1, 2, 3, 4, 5])
+        sort_hidden(7, 0, 3, "vector")
+        quantize_hidden(6)
+        quantize_post(6)
+        add_bias(6, nc.gpsimd)
+        turn_hidden(7, 0)
+        turn_hidden(7, 1)
+        finish(5)
+        weigh(8)
+        turn_post(7)
+        exponentiate(9)
+        multiply(6, [0, 1, 2, 3, 4, 5])
+        sort_hidden(8, 0, 3, "vector")
+        quantize_hidden(7)
+        quantize_post(7)
+        add_bias(7, nc.gpsimd)
+        turn_hidden(8, 0)
+        turn_hidden(8, 1)
+        finish(6)
+        weigh(9)
+        turn_post(8)
+        exponentiate(10)
+        multiply(7, [0, 1, 2, 3, 4, 5])
+        sort_hidden(9, 0, 3, "vector")
+        quantize_hidden(8)
+        quantize_post(8)
+        add_bias(8, nc.gpsimd)
+        turn_hidden(9, 0)
+        turn_hidden(9, 1)
+        finish(7)
+        weigh(10)
+        turn_post(9)
+        exponentiate(11)
+        multiply(8, [0, 1, 2, 3, 4, 5])
+        sort_hidden(10, 0, 3, "vector")
+        quantize_hidden(9)
+        quantize_post(9)
+        add_bias(9, nc.gpsimd)
+        turn_hidden(10, 0)
+        turn_hidden(10, 1)
+        finish(8)
+        weigh(11)
+        turn_post(10)
+        exponentiate(12)
+        multiply(9, [0, 1, 2, 3, 4, 5])
+        sort_hidden(11, 0, 3, "vector")
+        quantize_hidden(10)
+        quantize_post(10)
+        add_bias(10, nc.gpsimd)
+        turn_hidden(11, 0)
+        turn_hidden(11, 1)
+        finish(9)
+        weigh(12)
+        turn_post(11)
+        exponentiate(13)
+        multiply(10, [0, 1, 2, 3, 4, 5])
+        sort_hidden(12, 0, 3, "vector")
+        quantize_hidden(11)
+        quantize_post(11)
+        add_bias(11, nc.gpsimd)
+        turn_hidden(12, 0)
+        turn_hidden(12, 1)
+        finish(10)
+        weigh(13)
+        turn_post(12)
+        exponentiate(14)
+        multiply(11, [0, 1, 2, 3, 4, 5])
+        sort_hidden(13, 0, 3, "vector")
+        quantize_hidden(12)
+        quantize_post(12)
+        add_bias(12, nc.gpsimd)
+        turn_hidden(13, 0)
+        turn_hidden(13, 1)
+        finish(11)
+        weigh(14)
+        turn_post(13)
+        exponentiate(15)
+        multiply(12, [0, 1, 2, 3, 4, 5])
+        sort_hidden(14, 0, 3, "vector")
+        quantize_hidden(13)
+        quantize_post(13)
+        add_bias(13, nc.gpsimd)
+        turn_hidden(14, 0)
+        turn_hidden(14, 1)
+        finish(12)
+        weigh(15)
+        turn_post(14)
+        multiply(13, [0, 1, 2, 3, 4, 5])
+        sort_hidden(15, 0, 3, "vector")
+        quantize_hidden(14)
+        quantize_post(14)
+        add_bias(14, nc.gpsimd)
+        turn_hidden(15, 0)
+        turn_hidden(15, 1)
+        finish(13)
+        turn_post(15)
+        multiply(14, [0, 1, 2, 3, 4, 5])
+        quantize_hidden(15)
+        quantize_post(15)
+        add_bias(15, nc.gpsimd)
+        finish(14)
+        multiply(15, [0, 1, 2, 3, 4, 5])
+        finish(15, 2)

@@ -39,7 +39,7 @@ def tile_self_conditioned_ctc_s2_kernel(tc, frames, hidden, w_out, logits, lse, 
         frame_rows = frames.rearrange("(p i) k -> p i k", i=TILES)
         out_rows = out.rearrange("(p i) k -> p i k", i=TILES)
 
-        hid, logi, frm, w_raw, done, sorted_words, sorted_tile = {}, {}, {}, {}, {}, {}, {}
+        hid, logi, frm, w_raw, done, sorted_words, post_bank = {}, {}, {}, {}, {}, {}, {}
         ex, post, hid_k, post_k, hid_q, post_q, w_k, w_q, acc, base = {}, {}, {}, {}, {}, {}, {}, {}, {}, {}
 
         def load_rows(store, rows, label, first, count):
@@ -104,15 +104,14 @@ def tile_self_conditioned_ctc_s2_kernel(tc, frames, hidden, w_out, logits, lse, 
             post[i] = t
 
         def sort_hidden(i, first, count, engine):
-            if i not in sorted_tile:
-                sorted_tile[i] = work.tile([P, F_PASSES, 2, P], F32, name="sorted", tag="w_k", bufs=3, align_bytes=64)
-            words = hid[i].bitcast(F32)[:, first * 256 : (first + count) * 256].rearrange("p (g c u) -> p g u c", g=count, u=2)
+            t = work.tile([P, 2, count * P], F32, name="sorted", tag="w_k", bufs=3, align_bytes=64)
+            words = hid[i].bitcast(F32)[:, first * 256 : (first + count) * 256].rearrange("p (c u) -> p u c", u=2)
             if engine == "scalar":
-                nc.scalar.copy(out=sorted_tile[i][:, first : first + count, :, :], in_=words)
+                nc.scalar.copy(out=t[:], in_=words)
             else:
-                nc.vector.tensor_copy(out=sorted_tile[i][:, first : first + count, :, :], in_=words)
-            for g in range(first, first + count):
-                sorted_words[i, g] = sorted_tile[i][:, g, :, :]
+                nc.vector.tensor_copy(out=t[:], in_=words)
+            for g in range(count):
+                sorted_words[i, first + g] = t[:, :, g * P : (g + 1) * P]
 
         def turn_hidden(i, half):
             words = hid[i].bitcast(F32)
@@ -130,7 +129,7 @@ def tile_self_conditioned_ctc_s2_kernel(tc, frames, hidden, w_out, logits, lse, 
             dst = hid_k[i][:, half * 1024 : (half + 1) * 1024].bitcast(F32)
             nc.scalar.copy(out=dst.rearrange("p (g r u) -> p g r u", g=2, u=2), in_=bank[:].rearrange("p g u r -> p g r u"))
 
-        def turn_post(i):
+        def turn_post(i, engine="scalar"):
             words = post[i][:].bitcast(F32)
             bank = transpose_bank()
             for g in range(2):
@@ -138,8 +137,17 @@ def tile_self_conditioned_ctc_s2_kernel(tc, frames, hidden, w_out, logits, lse, 
                     first = u * 256 + g * P
                     nc.tensor.transpose(bank[:, g, u, :], words[:, first : first + P], ident[:])
             post_k[i] = keep.tile([P, V], BF16, name="post_k", tag="shared%d" % (i % 4), align_bytes=64)
-            dst = post_k[i][:].bitcast(F32)
-            nc.scalar.copy(out=dst.rearrange("p (g r u) -> p g r u", g=2, u=2), in_=bank[:].rearrange("p g u r -> p g r u"))
+            post_bank[i] = bank
+            if engine == "scalar":
+                empty_post(i, engine)
+
+        def empty_post(i, engine):
+            dst = post_k[i][:].bitcast(F32).rearrange("p (g r u) -> p g r u", g=2, u=2)
+            src = post_bank[i][:].rearrange("p g u r -> p g r u")
+            if engine == "scalar":
+                nc.scalar.copy(out=dst, in_=src)
+            else:
+                nc.vector.tensor_copy(out=dst, in_=src)
 
         def quantize_hidden(i):
             codes = work.tile([P, F // PACK], U32, name="hid_codes", bufs=QBUFS, align_bytes=64)
@@ -184,6 +192,11 @@ def tile_self_conditioned_ctc_s2_kernel(tc, frames, hidden, w_out, logits, lse, 
                 nc.vector.tensor_tensor(out=res[:, c : c + width], in0=acc[i][:, c : c + width], in1=base[i][:, c : c + width], op=ADD)
                 nc.sync.dma_start(out=out_rows[:, i, c : c + width], in_=res[:, c : c + width])
 
+        warm = keep.tile([P, 1], F32, name="warm")
+        warm_out = keep.tile([P, 1], F32, name="warm_out")
+        nc.vector.memset(warm[:], 0.0)
+        nc.scalar.activation(out=warm_out[:], in_=warm[:], func=EXP)
+
         ident = keep.tile([P, P], F32, name="ident", align_bytes=64)
         make_identity(nc, ident[:])
 
@@ -195,24 +208,24 @@ def tile_self_conditioned_ctc_s2_kernel(tc, frames, hidden, w_out, logits, lse, 
         bias_all = keep.tile([P, D], BF16, name="bias_all", align_bytes=64)
 
         nc.sync.dma_start(out=lse_sb[:], in_=lse.rearrange("(p i) -> p i", i=TILES))
-        nc.sync.dma_start(out=gain_sb[:], in_=gain.rearrange("(g p m) -> p g m", g=2, m=4))
         load_rows(logi, logit_rows, "logi", 0, 1)
+        nc.sync.dma_start(out=gain_sb[:], in_=gain.rearrange("(g p m) -> p g m", g=2, m=4))
         load_rows(hid, hidden_rows, "hid", 0, 1)
-        load_weight(0)
         load_rows(logi, logit_rows, "logi", 1, 1)
+        load_weight(0)
         load_weight(1)
-        load_rows(hid, hidden_rows, "hid", 1, 1)
         load_rows(logi, logit_rows, "logi", 2, 1)
+        load_rows(hid, hidden_rows, "hid", 1, 1)
         load_weight(2)
         load_weight(3)
-        load_rows(hid, hidden_rows, "hid", 2, 1)
-        nc.sync.dma_start(out=bias_sb[:], in_=bias.rearrange("(p m) -> p m", m=4))
-        load_weight(4)
         load_rows(logi, logit_rows, "logi", 3, 1)
+        load_rows(hid, hidden_rows, "hid", 2, 1)
+        load_weight(4)
         load_weight(5)
+        nc.sync.dma_start(out=bias_sb[:], in_=bias.rearrange("(p m) -> p m", m=4))
+        load_rows(logi, logit_rows, "logi", 4, 1)
         load_rows(hid, hidden_rows, "hid", 3, 1)
         load_rows(frm, frame_rows, "frm", 0, 4)
-        load_rows(logi, logit_rows, "logi", 4, 1)
         load_rows(hid, hidden_rows, "hid", 4, 1)
         load_rows(logi, logit_rows, "logi", 5, 1)
         load_rows(hid, hidden_rows, "hid", 5, 1)
@@ -232,27 +245,28 @@ def tile_self_conditioned_ctc_s2_kernel(tc, frames, hidden, w_out, logits, lse, 
         nc.vector.tensor_scalar(out=neg_lse[:], in0=lse_sb[:], scalar1=-1.0, scalar2=None, op0=MULT)
         exponentiate(0)
         spread_gain()
+        exponentiate(1)
         weigh(0)
         turn_hidden(0, 0)
         turn_hidden(0, 1)
-        exponentiate(1)
-        interleave_weight(0, "vector")
-        interleave_weight(1, "vector", 0, 256)
         weigh(1)
         turn_post(0)
-        interleave_weight(1, "scalar", 256, 512)
+        interleave_weight(0, "vector")
+        interleave_weight(1, "vector", 0, 128)
+        interleave_weight(1, "scalar", 128, 512)
+        exponentiate(2)
         quantize_hidden(0)
         quantize_weight(0)
         quantize_post(0)
         quantize_weight(1)
         turn_hidden(1, 0)
         turn_hidden(1, 1)
-        exponentiate(2)
-        interleave_weight(2, "vector")
-        interleave_weight(3, "vector", 0, 256)
         weigh(2)
         turn_post(1)
-        interleave_weight(3, "scalar", 256, 512)
+        interleave_weight(2, "vector")
+        interleave_weight(3, "vector", 0, 128)
+        interleave_weight(3, "scalar", 128, 512)
+        exponentiate(3)
         multiply(0, [0, 1])
         quantize_hidden(1)
         quantize_weight(2)
@@ -261,12 +275,12 @@ def tile_self_conditioned_ctc_s2_kernel(tc, frames, hidden, w_out, logits, lse, 
         turn_hidden(2, 0)
         turn_hidden(2, 1)
         spread_bias()
-        exponentiate(3)
-        interleave_weight(4, "vector")
-        interleave_weight(5, "vector", 0, 256)
         weigh(3)
         turn_post(2)
-        interleave_weight(5, "scalar", 256, 512)
+        interleave_weight(4, "vector")
+        interleave_weight(5, "vector", 0, 128)
+        interleave_weight(5, "scalar", 128, 512)
+        exponentiate(4)
         multiply(0, [2, 3])
         multiply(1, [0, 1, 2, 3])
         quantize_hidden(2)
@@ -278,7 +292,6 @@ def tile_self_conditioned_ctc_s2_kernel(tc, frames, hidden, w_out, logits, lse, 
         add_bias(2, nc.vector)
         turn_hidden(3, 0)
         turn_hidden(3, 1)
-        exponentiate(4)
         weigh(4)
         turn_post(3)
         exponentiate(5)
@@ -295,7 +308,6 @@ def tile_self_conditioned_ctc_s2_kernel(tc, frames, hidden, w_out, logits, lse, 
         turn_post(4)
         exponentiate(6)
         multiply(3, [0, 1, 2, 3, 4, 5])
-        sort_hidden(5, 0, 3, "vector")
         quantize_hidden(4)
         quantize_post(4)
         add_bias(4, nc.gpsimd)
@@ -305,10 +317,11 @@ def tile_self_conditioned_ctc_s2_kernel(tc, frames, hidden, w_out, logits, lse, 
         turn_hidden(5, 1)
         finish(3)
         weigh(6)
-        turn_post(5)
+        turn_post(5, "vector")
+        empty_post(5, "vector")
+        sort_hidden(6, 0, 3, "scalar")
         exponentiate(7)
         multiply(4, [0, 1, 2, 3, 4, 5])
-        sort_hidden(6, 0, 3, "vector")
         quantize_hidden(5)
         quantize_post(5)
         add_bias(5, nc.gpsimd)
@@ -316,10 +329,11 @@ def tile_self_conditioned_ctc_s2_kernel(tc, frames, hidden, w_out, logits, lse, 
         turn_hidden(6, 1)
         finish(4)
         weigh(7)
-        turn_post(6)
+        turn_post(6, "vector")
+        empty_post(6, "vector")
+        sort_hidden(7, 0, 3, "scalar")
         exponentiate(8)
         multiply(5, [0, 1, 2, 3, 4, 5])
-        sort_hidden(7, 0, 3, "vector")
         quantize_hidden(6)
         quantize_post(6)
         add_bias(6, nc.gpsimd)
@@ -327,10 +341,11 @@ def tile_self_conditioned_ctc_s2_kernel(tc, frames, hidden, w_out, logits, lse, 
         turn_hidden(7, 1)
         finish(5)
         weigh(8)
-        turn_post(7)
+        turn_post(7, "vector")
+        empty_post(7, "vector")
+        sort_hidden(8, 0, 3, "scalar")
         exponentiate(9)
         multiply(6, [0, 1, 2, 3, 4, 5])
-        sort_hidden(8, 0, 3, "vector")
         quantize_hidden(7)
         quantize_post(7)
         add_bias(7, nc.gpsimd)
@@ -338,10 +353,11 @@ def tile_self_conditioned_ctc_s2_kernel(tc, frames, hidden, w_out, logits, lse, 
         turn_hidden(8, 1)
         finish(6)
         weigh(9)
-        turn_post(8)
+        turn_post(8, "vector")
+        empty_post(8, "vector")
+        sort_hidden(9, 0, 3, "scalar")
         exponentiate(10)
         multiply(7, [0, 1, 2, 3, 4, 5])
-        sort_hidden(9, 0, 3, "vector")
         quantize_hidden(8)
         quantize_post(8)
         add_bias(8, nc.gpsimd)
@@ -349,10 +365,11 @@ def tile_self_conditioned_ctc_s2_kernel(tc, frames, hidden, w_out, logits, lse, 
         turn_hidden(9, 1)
         finish(7)
         weigh(10)
-        turn_post(9)
+        turn_post(9, "vector")
+        empty_post(9, "vector")
+        sort_hidden(10, 0, 3, "scalar")
         exponentiate(11)
         multiply(8, [0, 1, 2, 3, 4, 5])
-        sort_hidden(10, 0, 3, "vector")
         quantize_hidden(9)
         quantize_post(9)
         add_bias(9, nc.gpsimd)
@@ -360,10 +377,11 @@ def tile_self_conditioned_ctc_s2_kernel(tc, frames, hidden, w_out, logits, lse, 
         turn_hidden(10, 1)
         finish(8)
         weigh(11)
-        turn_post(10)
+        turn_post(10, "vector")
+        empty_post(10, "vector")
+        sort_hidden(11, 0, 3, "scalar")
         exponentiate(12)
         multiply(9, [0, 1, 2, 3, 4, 5])
-        sort_hidden(11, 0, 3, "vector")
         quantize_hidden(10)
         quantize_post(10)
         add_bias(10, nc.gpsimd)
@@ -371,10 +389,11 @@ def tile_self_conditioned_ctc_s2_kernel(tc, frames, hidden, w_out, logits, lse, 
         turn_hidden(11, 1)
         finish(9)
         weigh(12)
-        turn_post(11)
+        turn_post(11, "vector")
+        empty_post(11, "vector")
+        sort_hidden(12, 0, 3, "scalar")
         exponentiate(13)
         multiply(10, [0, 1, 2, 3, 4, 5])
-        sort_hidden(12, 0, 3, "vector")
         quantize_hidden(11)
         quantize_post(11)
         add_bias(11, nc.gpsimd)
@@ -382,10 +401,11 @@ def tile_self_conditioned_ctc_s2_kernel(tc, frames, hidden, w_out, logits, lse, 
         turn_hidden(12, 1)
         finish(10)
         weigh(13)
-        turn_post(12)
+        turn_post(12, "vector")
+        empty_post(12, "vector")
+        sort_hidden(13, 0, 3, "scalar")
         exponentiate(14)
         multiply(11, [0, 1, 2, 3, 4, 5])
-        sort_hidden(13, 0, 3, "vector")
         quantize_hidden(12)
         quantize_post(12)
         add_bias(12, nc.gpsimd)
@@ -393,10 +413,11 @@ def tile_self_conditioned_ctc_s2_kernel(tc, frames, hidden, w_out, logits, lse, 
         turn_hidden(13, 1)
         finish(11)
         weigh(14)
-        turn_post(13)
+        turn_post(13, "vector")
+        empty_post(13, "vector")
+        sort_hidden(14, 0, 3, "scalar")
         exponentiate(15)
         multiply(12, [0, 1, 2, 3, 4, 5])
-        sort_hidden(14, 0, 3, "vector")
         quantize_hidden(13)
         quantize_post(13)
         add_bias(13, nc.gpsimd)
@@ -404,9 +425,10 @@ def tile_self_conditioned_ctc_s2_kernel(tc, frames, hidden, w_out, logits, lse, 
         turn_hidden(14, 1)
         finish(12)
         weigh(15)
-        turn_post(14)
+        turn_post(14, "vector")
+        empty_post(14, "vector")
+        sort_hidden(15, 0, 3, "scalar")
         multiply(13, [0, 1, 2, 3, 4, 5])
-        sort_hidden(15, 0, 3, "vector")
         quantize_hidden(14)
         quantize_post(14)
         add_bias(14, nc.gpsimd)

@@ -22,7 +22,7 @@ K_PASS = P * PACK
 TILES = T // P
 F_PASSES = F // K_PASS
 V_PASSES = V // K_PASS
-QBUFS = 4
+QBUFS = 3
 TBANKS = 4
 
 
@@ -181,7 +181,8 @@ def tile_self_conditioned_ctc_s2_kernel(tc, frames, hidden, w_out, logits, lse, 
                 )
 
         def add_bias(i, engine):
-            base[i] = keep.tile([P, D], F32, name="base", tag="shared%d" % (i % 4), align_bytes=64)
+            tag = "shared%d" % {0: 2, 2: 4}.get(i, i % 4)
+            base[i] = keep.tile([P, D], F32, name="base", tag=tag, align_bytes=64)
             engine.tensor_tensor(out=base[i][:], in0=frm[i], in1=bias_all[:], op=ADD)
 
         def finish(i, parts=1):
@@ -210,19 +211,19 @@ def tile_self_conditioned_ctc_s2_kernel(tc, frames, hidden, w_out, logits, lse, 
         nc.sync.dma_start(out=lse_sb[:], in_=lse.rearrange("(p i) -> p i", i=TILES))
         load_rows(logi, logit_rows, "logi", 0, 1)
         nc.sync.dma_start(out=gain_sb[:], in_=gain.rearrange("(g p m) -> p g m", g=2, m=4))
-        load_rows(hid, hidden_rows, "hid", 0, 1)
         load_rows(logi, logit_rows, "logi", 1, 1)
+        load_rows(hid, hidden_rows, "hid", 0, 1)
         load_weight(0)
         load_weight(1)
         load_rows(logi, logit_rows, "logi", 2, 1)
         load_rows(hid, hidden_rows, "hid", 1, 1)
+        nc.sync.dma_start(out=bias_sb[:], in_=bias.rearrange("(p m) -> p m", m=4))
         load_weight(2)
         load_weight(3)
         load_rows(logi, logit_rows, "logi", 3, 1)
         load_rows(hid, hidden_rows, "hid", 2, 1)
         load_weight(4)
         load_weight(5)
-        nc.sync.dma_start(out=bias_sb[:], in_=bias.rearrange("(p m) -> p m", m=4))
         load_rows(logi, logit_rows, "logi", 4, 1)
         load_rows(hid, hidden_rows, "hid", 3, 1)
         load_rows(frm, frame_rows, "frm", 0, 4)
@@ -257,47 +258,57 @@ def tile_self_conditioned_ctc_s2_kernel(tc, frames, hidden, w_out, logits, lse, 
         exponentiate(2)
         quantize_hidden(0)
         quantize_weight(0)
-        quantize_post(0)
         quantize_weight(1)
+        quantize_post(0)
         turn_hidden(1, 0)
         turn_hidden(1, 1)
         weigh(2)
         turn_post(1)
+        quantize_hidden(1)
         interleave_weight(2, "vector")
         interleave_weight(3, "vector", 0, 128)
         interleave_weight(3, "scalar", 128, 512)
         exponentiate(3)
-        multiply(0, [0, 1])
-        quantize_hidden(1)
+        multiply(0, [0])
+        multiply(0, [1])
         quantize_weight(2)
-        quantize_post(1)
         quantize_weight(3)
+        quantize_post(1)
         turn_hidden(2, 0)
         turn_hidden(2, 1)
         spread_bias()
         weigh(3)
         turn_post(2)
+        quantize_hidden(2)
         interleave_weight(4, "vector")
         interleave_weight(5, "vector", 0, 128)
         interleave_weight(5, "scalar", 128, 512)
         exponentiate(4)
-        multiply(0, [2, 3])
-        multiply(1, [0, 1, 2, 3])
-        quantize_hidden(2)
+        multiply(1, [0])
+        multiply(1, [1])
+        multiply(0, [2])
+        multiply(1, [2])
+        multiply(0, [3])
+        multiply(1, [3])
         quantize_weight(4)
-        quantize_post(2)
         quantize_weight(5)
-        add_bias(0, nc.vector)
-        add_bias(1, nc.vector)
-        add_bias(2, nc.vector)
+        quantize_post(2)
+        add_bias(0, nc.gpsimd)
         turn_hidden(3, 0)
         turn_hidden(3, 1)
         weigh(4)
         turn_post(3)
         exponentiate(5)
-        multiply(0, [4, 5])
-        multiply(1, [4, 5])
-        multiply(2, [0, 1, 2, 3, 4, 5])
+        multiply(2, [0])
+        multiply(2, [1])
+        multiply(2, [2])
+        multiply(2, [3])
+        multiply(0, [4])
+        multiply(1, [4])
+        multiply(2, [4])
+        multiply(0, [5])
+        multiply(1, [5])
+        multiply(2, [5])
         quantize_hidden(3)
         quantize_post(3)
         add_bias(3, nc.gpsimd)
@@ -307,7 +318,14 @@ def tile_self_conditioned_ctc_s2_kernel(tc, frames, hidden, w_out, logits, lse, 
         weigh(5)
         turn_post(4)
         exponentiate(6)
-        multiply(3, [0, 1, 2, 3, 4, 5])
+        multiply(3, [0])
+        multiply(3, [1])
+        multiply(3, [2])
+        multiply(3, [3])
+        multiply(3, [4])
+        multiply(3, [5])
+        add_bias(1, nc.vector)
+        add_bias(2, nc.vector)
         quantize_hidden(4)
         quantize_post(4)
         add_bias(4, nc.gpsimd)
@@ -317,11 +335,15 @@ def tile_self_conditioned_ctc_s2_kernel(tc, frames, hidden, w_out, logits, lse, 
         turn_hidden(5, 1)
         finish(3)
         weigh(6)
-        turn_post(5, "vector")
-        empty_post(5, "vector")
-        sort_hidden(6, 0, 3, "scalar")
+        turn_post(5)
+        sort_hidden(6, 2, 1, "scalar")
         exponentiate(7)
-        multiply(4, [0, 1, 2, 3, 4, 5])
+        multiply(4, [0])
+        multiply(4, [1])
+        multiply(4, [2])
+        multiply(4, [3])
+        multiply(4, [4])
+        multiply(4, [5])
         quantize_hidden(5)
         quantize_post(5)
         add_bias(5, nc.gpsimd)
@@ -329,11 +351,16 @@ def tile_self_conditioned_ctc_s2_kernel(tc, frames, hidden, w_out, logits, lse, 
         turn_hidden(6, 1)
         finish(4)
         weigh(7)
-        turn_post(6, "vector")
-        empty_post(6, "vector")
-        sort_hidden(7, 0, 3, "scalar")
+        turn_post(6)
+        sort_hidden(7, 2, 1, "scalar")
         exponentiate(8)
-        multiply(5, [0, 1, 2, 3, 4, 5])
+        multiply(5, [0])
+        multiply(5, [1])
+        multiply(5, [2])
+        multiply(5, [3])
+        multiply(5, [4])
+        multiply(5, [5])
+        sort_hidden(7, 0, 2, "vector")
         quantize_hidden(6)
         quantize_post(6)
         add_bias(6, nc.gpsimd)
@@ -341,11 +368,16 @@ def tile_self_conditioned_ctc_s2_kernel(tc, frames, hidden, w_out, logits, lse, 
         turn_hidden(7, 1)
         finish(5)
         weigh(8)
-        turn_post(7, "vector")
-        empty_post(7, "vector")
-        sort_hidden(8, 0, 3, "scalar")
+        turn_post(7)
+        sort_hidden(8, 2, 1, "scalar")
         exponentiate(9)
-        multiply(6, [0, 1, 2, 3, 4, 5])
+        multiply(6, [0])
+        multiply(6, [1])
+        multiply(6, [2])
+        multiply(6, [3])
+        multiply(6, [4])
+        multiply(6, [5])
+        sort_hidden(8, 0, 2, "vector")
         quantize_hidden(7)
         quantize_post(7)
         add_bias(7, nc.gpsimd)
@@ -353,11 +385,16 @@ def tile_self_conditioned_ctc_s2_kernel(tc, frames, hidden, w_out, logits, lse, 
         turn_hidden(8, 1)
         finish(6)
         weigh(9)
-        turn_post(8, "vector")
-        empty_post(8, "vector")
-        sort_hidden(9, 0, 3, "scalar")
+        turn_post(8)
+        sort_hidden(9, 2, 1, "scalar")
         exponentiate(10)
-        multiply(7, [0, 1, 2, 3, 4, 5])
+        multiply(7, [0])
+        multiply(7, [1])
+        multiply(7, [2])
+        multiply(7, [3])
+        multiply(7, [4])
+        multiply(7, [5])
+        sort_hidden(9, 0, 2, "vector")
         quantize_hidden(8)
         quantize_post(8)
         add_bias(8, nc.gpsimd)
@@ -365,11 +402,16 @@ def tile_self_conditioned_ctc_s2_kernel(tc, frames, hidden, w_out, logits, lse, 
         turn_hidden(9, 1)
         finish(7)
         weigh(10)
-        turn_post(9, "vector")
-        empty_post(9, "vector")
-        sort_hidden(10, 0, 3, "scalar")
+        turn_post(9)
+        sort_hidden(10, 2, 1, "scalar")
         exponentiate(11)
-        multiply(8, [0, 1, 2, 3, 4, 5])
+        multiply(8, [0])
+        multiply(8, [1])
+        multiply(8, [2])
+        multiply(8, [3])
+        multiply(8, [4])
+        multiply(8, [5])
+        sort_hidden(10, 0, 2, "vector")
         quantize_hidden(9)
         quantize_post(9)
         add_bias(9, nc.gpsimd)
@@ -377,11 +419,16 @@ def tile_self_conditioned_ctc_s2_kernel(tc, frames, hidden, w_out, logits, lse, 
         turn_hidden(10, 1)
         finish(8)
         weigh(11)
-        turn_post(10, "vector")
-        empty_post(10, "vector")
-        sort_hidden(11, 0, 3, "scalar")
+        turn_post(10)
+        sort_hidden(11, 2, 1, "scalar")
         exponentiate(12)
-        multiply(9, [0, 1, 2, 3, 4, 5])
+        multiply(9, [0])
+        multiply(9, [1])
+        multiply(9, [2])
+        multiply(9, [3])
+        multiply(9, [4])
+        multiply(9, [5])
+        sort_hidden(11, 0, 2, "vector")
         quantize_hidden(10)
         quantize_post(10)
         add_bias(10, nc.gpsimd)
@@ -389,11 +436,16 @@ def tile_self_conditioned_ctc_s2_kernel(tc, frames, hidden, w_out, logits, lse, 
         turn_hidden(11, 1)
         finish(9)
         weigh(12)
-        turn_post(11, "vector")
-        empty_post(11, "vector")
-        sort_hidden(12, 0, 3, "scalar")
+        turn_post(11)
+        sort_hidden(12, 2, 1, "scalar")
         exponentiate(13)
-        multiply(10, [0, 1, 2, 3, 4, 5])
+        multiply(10, [0])
+        multiply(10, [1])
+        multiply(10, [2])
+        multiply(10, [3])
+        multiply(10, [4])
+        multiply(10, [5])
+        sort_hidden(12, 0, 2, "vector")
         quantize_hidden(11)
         quantize_post(11)
         add_bias(11, nc.gpsimd)
@@ -401,11 +453,16 @@ def tile_self_conditioned_ctc_s2_kernel(tc, frames, hidden, w_out, logits, lse, 
         turn_hidden(12, 1)
         finish(10)
         weigh(13)
-        turn_post(12, "vector")
-        empty_post(12, "vector")
-        sort_hidden(13, 0, 3, "scalar")
+        turn_post(12)
+        sort_hidden(13, 2, 1, "scalar")
         exponentiate(14)
-        multiply(11, [0, 1, 2, 3, 4, 5])
+        multiply(11, [0])
+        multiply(11, [1])
+        multiply(11, [2])
+        multiply(11, [3])
+        multiply(11, [4])
+        multiply(11, [5])
+        sort_hidden(13, 0, 2, "vector")
         quantize_hidden(12)
         quantize_post(12)
         add_bias(12, nc.gpsimd)
@@ -413,11 +470,16 @@ def tile_self_conditioned_ctc_s2_kernel(tc, frames, hidden, w_out, logits, lse, 
         turn_hidden(13, 1)
         finish(11)
         weigh(14)
-        turn_post(13, "vector")
-        empty_post(13, "vector")
-        sort_hidden(14, 0, 3, "scalar")
+        turn_post(13)
+        sort_hidden(14, 2, 1, "scalar")
         exponentiate(15)
-        multiply(12, [0, 1, 2, 3, 4, 5])
+        multiply(12, [0])
+        multiply(12, [1])
+        multiply(12, [2])
+        multiply(12, [3])
+        multiply(12, [4])
+        multiply(12, [5])
+        sort_hidden(14, 0, 2, "vector")
         quantize_hidden(13)
         quantize_post(13)
         add_bias(13, nc.gpsimd)
@@ -425,10 +487,15 @@ def tile_self_conditioned_ctc_s2_kernel(tc, frames, hidden, w_out, logits, lse, 
         turn_hidden(14, 1)
         finish(12)
         weigh(15)
-        turn_post(14, "vector")
-        empty_post(14, "vector")
-        sort_hidden(15, 0, 3, "scalar")
-        multiply(13, [0, 1, 2, 3, 4, 5])
+        turn_post(14)
+        sort_hidden(15, 2, 1, "scalar")
+        multiply(13, [0])
+        multiply(13, [1])
+        multiply(13, [2])
+        multiply(13, [3])
+        multiply(13, [4])
+        multiply(13, [5])
+        sort_hidden(15, 0, 2, "vector")
         quantize_hidden(14)
         quantize_post(14)
         add_bias(14, nc.gpsimd)
@@ -436,10 +503,20 @@ def tile_self_conditioned_ctc_s2_kernel(tc, frames, hidden, w_out, logits, lse, 
         turn_hidden(15, 1)
         finish(13)
         turn_post(15)
-        multiply(14, [0, 1, 2, 3, 4, 5])
+        multiply(14, [0])
+        multiply(14, [1])
+        multiply(14, [2])
+        multiply(14, [3])
+        multiply(14, [4])
+        multiply(14, [5])
         quantize_hidden(15)
         quantize_post(15)
         add_bias(15, nc.gpsimd)
         finish(14)
-        multiply(15, [0, 1, 2, 3, 4, 5])
+        multiply(15, [0])
+        multiply(15, [1])
+        multiply(15, [2])
+        multiply(15, [3])
+        multiply(15, [4])
+        multiply(15, [5])
         finish(15, 2)

from contextlib import ExitStack

import concourse.mybir as mybir
from concourse.masks import make_identity

T, F, V, D = 2048, 2048, 1024, 512
FLOPS = 2 * T * (F + V) * D

F32 = mybir.dt.float32
BF16 = mybir.dt.bfloat16
U32 = mybir.dt.uint32
U8 = mybir.dt.uint8
E4M3 = mybir.dt.float8_e4m3fn_x4
E5M2 = mybir.dt.float8_e5m2_x4
ADD = mybir.AluOpType.add
MULT = mybir.AluOpType.mult
EXP = mybir.ActivationFunctionType.Exp

P = 128
PACK = 4
K_PASS = P * PACK
TILES = T // P
F_PASSES = F // K_PASS
V_PASSES = V // K_PASS
QBUFS = 3
TBANKS = 4


def tile_self_conditioned_ctc_s2_kernel(tc, frames, hidden, w_out, logits, lse, gain, w_back, bias, out):
    nc = tc.nc
    with ExitStack() as ctx:
        keep = ctx.enter_context(tc.tile_pool(name="keep", bufs=1))
        work = ctx.enter_context(tc.tile_pool(name="work", bufs=2))
        psum = ctx.enter_context(tc.psum_pool(name="psum", bufs=1))
        ctx.enter_context(tc.manual_schedule())

        hidden_rows = hidden.rearrange("(p i) k -> p i k", i=TILES)
        logit_rows = logits.rearrange("(p i) k -> p i k", i=TILES)
        frame_rows = frames.rearrange("(p i) k -> p i k", i=TILES)
        out_rows = out.rearrange("(p i) k -> p i k", i=TILES)

        hid, logi, frm, w_raw, done, sorted_words, post_bank = {}, {}, {}, {}, {}, {}, {}
        ex, post, hid_k, post_k, hid_q, post_q, w_k, w_q, acc, base = {}, {}, {}, {}, {}, {}, {}, {}, {}, {}

        def load_rows(store, rows, label, first, count):
            width = rows.shape[2]
            t = keep.tile([P, count, width], BF16, name="%s%d" % (label, first), align_bytes=64)
            nc.sync.dma_start(out=t[:], in_=rows[:, first : first + count, :])
            for j in range(count):
                store[first + j] = t[:, j, :]

        def load_weight(g):
            src = w_out[g * K_PASS : (g + 1) * K_PASS, :] if g < F_PASSES else w_back[(g - F_PASSES) * K_PASS : (g - F_PASSES + 1) * K_PASS, :]
            t = keep.tile([P, PACK, D], BF16, name="w_raw", tag="w_raw%d" % g, align_bytes=64)
            nc.sync.dma_start(out=t[:], in_=src.rearrange("(p j) n -> p j n", j=PACK))
            w_raw[g] = t

        def interleave_weight(g, engine, first=0, last=D):
            if g not in w_k:
                w_k[g] = work.tile([P, D, PACK], BF16, name="w_k", bufs=3, align_bytes=64)
            dst = w_k[g][:, first:last, :].rearrange("p (c i) j -> p c j i", i=4)
            src = w_raw[g][:, :, first:last].rearrange("p j (c i) -> p c j i", i=4)
            if engine == "scalar":
                nc.scalar.copy(out=dst, in_=src)
            else:
                nc.vector.tensor_copy(out=dst, in_=src)

        def quantize_weight(g):
            codes = keep.tile([P, D], U32, name="w_codes%d" % g, align_bytes=64)
            scales = keep.tile([P, D], U8, name="w_scales%d" % g, align_bytes=64)
            nc.vector.quantize_mx(out=codes[:].bitcast(E4M3), scales=scales[:], in_=w_k[g][:].rearrange("p n j -> p (n j)"))
            w_q[g] = (codes, scales)

        def transpose_bank():
            return psum.tile([P, 2, 2, P], F32, name="turned", bufs=TBANKS)

        def spread_gain():
            words = gain_sb[:].rearrange("p g m -> p (g m)").bitcast(F32)
            for u in range(2):
                for g in range(2):
                    col = 2 * g + u
                    nc.tensor.transpose(gain_bank[:, u, g, :], words[:, col : col + 1].to_broadcast([P, P]), ident[:])

        def spread_bias():
            words = bias_sb[:].bitcast(F32)
            bank = transpose_bank()
            for a in range(2):
                nc.tensor.transpose(bank[:, 0, a, :], words[:, a : a + 1].to_broadcast([P, P]), ident[:])
            nc.scalar.copy(out=bias_all[:].bitcast(F32).rearrange("p (n a) -> p n a", a=2), in_=bank[:, 0, :, :].rearrange("p a n -> p n a"))

        def exponentiate(i):
            t = work.tile([P, V], F32, name="ex", bufs=2, align_bytes=64)
            nc.scalar.activation(
                out=t[:].rearrange("p (u c e) -> p u c e", u=2, e=2),
                in_=logi[i].rearrange("p (c u e) -> p u c e", u=2, e=2),
                func=EXP,
                bias=neg_lse[:, i : i + 1],
            )
            ex[i] = t

        def weigh(i):
            t = work.tile([P, V], BF16, name="post", bufs=3, align_bytes=64)
            nc.vector.tensor_tensor(out=t[:], in0=ex[i][:], in1=gain_bank[:].rearrange("p u g n -> p (u g n)").bitcast(BF16), op=MULT)
            post[i] = t

        def sort_hidden(i, first, count, engine):
            t = work.tile([P, 2, count * P], F32, name="sorted", tag="w_k", bufs=3, align_bytes=64)
            words = hid[i].bitcast(F32)[:, first * 256 : (first + count) * 256].rearrange("p (c u) -> p u c", u=2)
            if engine == "scalar":
                nc.scalar.copy(out=t[:], in_=words)
            else:
                nc.vector.tensor_copy(out=t[:], in_=words)
            for g in range(count):
                sorted_words[i, first + g] = t[:, :, g * P : (g + 1) * P]

        def turn_hidden(i, half):
            words = hid[i].bitcast(F32)
            bank = transpose_bank()
            for g in range(2):
                first = (2 * half + g) * 256
                for u in range(2):
                    if (i, 2 * half + g) in sorted_words:
                        src = sorted_words[i, 2 * half + g][:, u, :]
                    else:
                        src = words[:, first + u : first + 256 : 2]
                    nc.tensor.transpose(bank[:, g, u, :], src, ident[:])
            if half == 0:
                hid_k[i] = work.tile([P, F], BF16, name="hid_k", bufs=2, align_bytes=64)
            dst = hid_k[i][:, half * 1024 : (half + 1) * 1024].bitcast(F32)
            nc.scalar.copy(out=dst.rearrange("p (g r u) -> p g r u", g=2, u=2), in_=bank[:].rearrange("p g u r -> p g r u"))

        def turn_post(i, engine="scalar"):
            words = post[i][:].bitcast(F32)
            bank = transpose_bank()
            for g in range(2):
                for u in range(2):
                    first = u * 256 + g * P
                    nc.tensor.transpose(bank[:, g, u, :], words[:, first : first + P], ident[:])
            post_k[i] = keep.tile([P, V], BF16, name="post_k", tag="shared%d" % (i % 4), align_bytes=64)
            post_bank[i] = bank
            if engine == "scalar":
                empty_post(i, engine)

        def empty_post(i, engine):
            dst = post_k[i][:].bitcast(F32).rearrange("p (g r u) -> p g r u", g=2, u=2)
            src = post_bank[i][:].rearrange("p g u r -> p g r u")
            if engine == "scalar":
                nc.scalar.copy(out=dst, in_=src)
            else:
                nc.vector.tensor_copy(out=dst, in_=src)

        def quantize_hidden(i):
            codes = work.tile([P, F // PACK], U32, name="hid_codes", bufs=QBUFS, align_bytes=64)
            scales = work.tile([P, F // PACK], U8, name="hid_scales", bufs=QBUFS, align_bytes=64)
            nc.vector.quantize_mx(out=codes[:].bitcast(E4M3), scales=scales[:], in_=hid_k[i][:])
            hid_q[i] = (codes, scales)

        def quantize_post(i):
            codes = work.tile([P, V // PACK], U32, name="post_codes", bufs=QBUFS, align_bytes=64)
            scales = work.tile([P, V // PACK], U8, name="post_scales", bufs=QBUFS, align_bytes=64)
            nc.vector.quantize_mx(out=codes[:].bitcast(E5M2), scales=scales[:], in_=post_k[i][:])
            post_q[i] = (codes, scales)

        def multiply(i, passes):
            for g in passes:
                done[i] = done.get(i, 0) + 1
                if done[i] == 1:
                    acc[i] = psum.tile([P, D], F32, name="acc", bufs=7 - TBANKS)
                if g < F_PASSES:
                    (codes, scales), fmt, c = hid_q[i], E4M3, g
                else:
                    (codes, scales), fmt, c = post_q[i], E5M2, g - F_PASSES
                nc.tensor.matmul_mx(
                    out=acc[i][:],
                    lhsT=codes[:, c * P : (c + 1) * P].bitcast(fmt),
                    lhsT_scale=scales[:, c * P : (c + 1) * P],
                    rhs=w_q[g][0][:].bitcast(E4M3),
                    rhs_scale=w_q[g][1][:],
                    start=(done[i] == 1),
                    stop=(done[i] == F_PASSES + V_PASSES),
                )

        def add_bias(i, engine):
            tag = "shared%d" % {0: 2, 2: 4}.get(i, i % 4)
            base[i] = keep.tile([P, D], F32, name="base", tag=tag, align_bytes=64)
            engine.tensor_tensor(out=base[i][:], in0=frm[i], in1=bias_all[:], op=ADD)

        def finish(i, parts=1):
            tag = "res%d" % i if i < TILES - 6 else "w_raw%d" % (i - TILES + 6)
            res = keep.tile([P, D], F32, name="res", tag=tag, align_bytes=64)
            width = D // parts
            for c in range(0, D, width):
                nc.vector.tensor_tensor(out=res[:, c : c + width], in0=acc[i][:, c : c + width], in1=base[i][:, c : c + width], op=ADD)
                nc.sync.dma_start(out=out_rows[:, i, c : c + width], in_=res[:, c : c + width])

        warm = keep.tile([P, 1], F32, name="warm")
        warm_out = keep.tile([P, 1], F32, name="warm_out")
        nc.vector.memset(warm[:], 0.0)
        nc.scalar.activation(out=warm_out[:], in_=warm[:], func=EXP)

        ident = keep.tile([P, P], F32, name="ident", align_bytes=64)
        make_identity(nc, ident[:])

        lse_sb = keep.tile([P, TILES], BF16, name="lse_sb")
        gain_sb = keep.tile([P, 2, 4], BF16, name="gain_sb")
        bias_sb = keep.tile([P, 4], BF16, name="bias_sb")
        neg_lse = keep.tile([P, TILES], F32, name="neg_lse")
        gain_bank = psum.tile([P, 2, 2, P], F32, name="gain_bank")
        bias_all = keep.tile([P, D], BF16, name="bias_all", align_bytes=64)

        nc.sync.dma_start(out=lse_sb[:], in_=lse.rearrange("(p i) -> p i", i=TILES))
        load_rows(logi, logit_rows, "logi", 0, 1)
        nc.sync.dma_start(out=gain_sb[:], in_=gain.rearrange("(g p m) -> p g m", g=2, m=4))
        load_rows(logi, logit_rows, "logi", 1, 1)
        load_rows(hid, hidden_rows, "hid", 0, 1)
        load_weight(0)
        load_weight(1)
        load_rows(logi, logit_rows, "logi", 2, 1)
        load_rows(hid, hidden_rows, "hid", 1, 1)
        nc.sync.dma_start(out=bias_sb[:], in_=bias.rearrange("(p m) -> p m", m=4))
        load_weight(2)
        load_weight(3)
        load_rows(logi, logit_rows, "logi", 3, 1)
        load_rows(hid, hidden_rows, "hid", 2, 1)
        load_weight(4)
        load_weight(5)
        load_rows(logi, logit_rows, "logi", 4, 1)
        load_rows(hid, hidden_rows, "hid", 3, 1)
        load_rows(frm, frame_rows, "frm", 0, 4)
        load_rows(hid, hidden_rows, "hid", 4, 1)
        load_rows(logi, logit_rows, "logi", 5, 1)
        load_rows(hid, hidden_rows, "hid", 5, 1)
        load_rows(frm, frame_rows, "frm", 4, 4)
        load_rows(logi, logit_rows, "logi", 6, 2)
        load_rows(hid, hidden_rows, "hid", 6, 2)
        load_rows(logi, logit_rows, "logi", 8, 2)
        load_rows(hid, hidden_rows, "hid", 8, 2)
        load_rows(frm, frame_rows, "frm", 8, 4)
        load_rows(logi, logit_rows, "logi", 10, 2)
        load_rows(hid, hidden_rows, "hid", 10, 2)
        load_rows(logi, logit_rows, "logi", 12, 2)
        load_rows(hid, hidden_rows, "hid", 12, 2)
        load_rows(frm, frame_rows, "frm", 12, 4)
        load_rows(logi, logit_rows, "logi", 14, 2)
        load_rows(hid, hidden_rows, "hid", 14, 2)
        nc.vector.tensor_scalar(out=neg_lse[:], in0=lse_sb[:], scalar1=-1.0, scalar2=None, op0=MULT)
        exponentiate(0)
        spread_gain()
        exponentiate(1)
        weigh(0)
        turn_hidden(0, 0)
        turn_hidden(0, 1)
        weigh(1)
        turn_post(0)
        interleave_weight(0, "vector")
        interleave_weight(1, "vector", 0, 128)
        interleave_weight(1, "scalar", 128, 512)
        exponentiate(2)
        quantize_hidden(0)
        quantize_weight(0)
        quantize_weight(1)
        quantize_post(0)
        turn_hidden(1, 0)
        turn_hidden(1, 1)
        weigh(2)
        turn_post(1)
        quantize_hidden(1)
        interleave_weight(2, "vector")
        interleave_weight(3, "vector", 0, 128)
        interleave_weight(3, "scalar", 128, 512)
        exponentiate(3)
        multiply(0, [0])
        multiply(0, [1])
        quantize_weight(2)
        quantize_weight(3)
        quantize_post(1)
        turn_hidden(2, 0)
        turn_hidden(2, 1)
        spread_bias()
        weigh(3)
        turn_post(2)
        quantize_hidden(2)
        interleave_weight(4, "vector")
        interleave_weight(5, "vector", 0, 128)
        interleave_weight(5, "scalar", 128, 512)
        exponentiate(4)
        multiply(1, [0])
        multiply(1, [1])
        multiply(0, [2])
        multiply(1, [2])
        multiply(0, [3])
        multiply(1, [3])
        quantize_weight(4)
        quantize_weight(5)
        quantize_post(2)
        add_bias(0, nc.gpsimd)
        turn_hidden(3, 0)
        turn_hidden(3, 1)
        weigh(4)
        turn_post(3)
        exponentiate(5)
        multiply(2, [0])
        multiply(2, [1])
        multiply(2, [2])
        multiply(2, [3])
        multiply(0, [4])
        multiply(1, [4])
        multiply(2, [4])
        multiply(0, [5])
        multiply(1, [5])
        multiply(2, [5])
        quantize_hidden(3)
        quantize_post(3)
        add_bias(3, nc.gpsimd)
        turn_hidden(4, 0)
        turn_hidden(4, 1)
        finish(0)
        weigh(5)
        turn_post(4)
        exponentiate(6)
        multiply(3, [0])
        multiply(3, [1])
        multiply(3, [2])
        multiply(3, [3])
        multiply(3, [4])
        multiply(3, [5])
        add_bias(1, nc.vector)
        add_bias(2, nc.vector)
        quantize_hidden(4)
        quantize_post(4)
        add_bias(4, nc.gpsimd)
        finish(1)
        finish(2)
        turn_hidden(5, 0)
        turn_hidden(5, 1)
        finish(3)
        weigh(6)
        turn_post(5)
        sort_hidden(6, 2, 1, "scalar")
        exponentiate(7)
        multiply(4, [0])
        multiply(4, [1])
        multiply(4, [2])
        multiply(4, [3])
        multiply(4, [4])
        multiply(4, [5])
        quantize_hidden(5)
        quantize_post(5)
        add_bias(5, nc.gpsimd)
        turn_hidden(6, 0)
        turn_hidden(6, 1)
        finish(4)
        weigh(7)
        turn_post(6)
        sort_hidden(7, 2, 1, "scalar")
        exponentiate(8)
        multiply(5, [0])
        multiply(5, [1])
        multiply(5, [2])
        multiply(5, [3])
        multiply(5, [4])
        multiply(5, [5])
        sort_hidden(7, 0, 2, "vector")
        quantize_hidden(6)
        quantize_post(6)
        add_bias(6, nc.gpsimd)
        turn_hidden(7, 0)
        turn_hidden(7, 1)
        finish(5)
        weigh(8)
        turn_post(7)
        sort_hidden(8, 2, 1, "scalar")
        exponentiate(9)
        multiply(6, [0])
        multiply(6, [1])
        multiply(6, [2])
        multiply(6, [3])
        multiply(6, [4])
        multiply(6, [5])
        sort_hidden(8, 0, 2, "vector")
        quantize_hidden(7)
        quantize_post(7)
        add_bias(7, nc.gpsimd)
        turn_hidden(8, 0)
        turn_hidden(8, 1)
        finish(6)
        weigh(9)
        turn_post(8)
        sort_hidden(9, 2, 1, "scalar")
        exponentiate(10)
        multiply(7, [0])
        multiply(7, [1])
        multiply(7, [2])
        multiply(7, [3])
        multiply(7, [4])
        multiply(7, [5])
        sort_hidden(9, 0, 2, "vector")
        quantize_hidden(8)
        quantize_post(8)
        add_bias(8, nc.gpsimd)
        turn_hidden(9, 0)
        turn_hidden(9, 1)
        finish(7)
        weigh(10)
        turn_post(9)
        sort_hidden(10, 2, 1, "scalar")
        exponentiate(11)
        multiply(8, [0])
        multiply(8, [1])
        multiply(8, [2])
        multiply(8, [3])
        multiply(8, [4])
        multiply(8, [5])
        sort_hidden(10, 0, 2, "vector")
        quantize_hidden(9)
        quantize_post(9)
        add_bias(9, nc.gpsimd)
        turn_hidden(10, 0)
        turn_hidden(10, 1)
        finish(8)
        weigh(11)
        turn_post(10)
        sort_hidden(11, 2, 1, "scalar")
        exponentiate(12)
        multiply(9, [0])
        multiply(9, [1])
        multiply(9, [2])
        multiply(9, [3])
        multiply(9, [4])
        multiply(9, [5])
        sort_hidden(11, 0, 2, "vector")
        quantize_hidden(10)
        quantize_post(10)
        add_bias(10, nc.gpsimd)
        turn_hidden(11, 0)
        turn_hidden(11, 1)
        finish(9)
        weigh(12)
        turn_post(11)
        sort_hidden(12, 2, 1, "scalar")
        exponentiate(13)
        multiply(10, [0])
        multiply(10, [1])
        multiply(10, [2])
        multiply(10, [3])
        multiply(10, [4])
        multiply(10, [5])
        sort_hidden(12, 0, 2, "vector")
        quantize_hidden(11)
        quantize_post(11)
        add_bias(11, nc.gpsimd)
        turn_hidden(12, 0)
        turn_hidden(12, 1)
        finish(10)
        weigh(13)
        turn_post(12)
        sort_hidden(13, 2, 1, "scalar")
        exponentiate(14)
        multiply(11, [0])
        multiply(11, [1])
        multiply(11, [2])
        multiply(11, [3])
        multiply(11, [4])
        multiply(11, [5])
        sort_hidden(13, 0, 2, "vector")
        quantize_hidden(12)
        quantize_post(12)
        add_bias(12, nc.gpsimd)
        turn_hidden(13, 0)
        turn_hidden(13, 1)
        finish(11)
        weigh(14)
        turn_post(13)
        sort_hidden(14, 2, 1, "scalar")
        exponentiate(15)
        multiply(12, [0])
        multiply(12, [1])
        multiply(12, [2])
        multiply(12, [3])
        multiply(12, [4])
        multiply(12, [5])
        sort_hidden(14, 0, 2, "vector")
        quantize_hidden(13)
        quantize_post(13)
        add_bias(13, nc.gpsimd)
        turn_hidden(14, 0)
        turn_hidden(14, 1)
        finish(12)
        weigh(15)
        turn_post(14)
        sort_hidden(15, 2, 1, "scalar")
        multiply(13, [0])
        multiply(13, [1])
        multiply(13, [2])
        multiply(13, [3])
        multiply(13, [4])
        multiply(13, [5])
        sort_hidden(15, 0, 2, "vector")
        quantize_hidden(14)
        quantize_post(14)
        add_bias(14, nc.gpsimd)
        turn_hidden(15, 0)
        turn_hidden(15, 1)
        finish(13)
        turn_post(15)
        multiply(14, [0])
        multiply(14, [1])
        multiply(14, [2])
        multiply(14, [3])
        multiply(14, [4])
        multiply(14, [5])
        quantize_hidden(15)
        quantize_post(15)
        add_bias(15, nc.gpsimd)
        finish(14)
        multiply(15, [0])
        multiply(15, [1])
        multiply(15, [2])
        multiply(15, [3])
        multiply(15, [4])
        multiply(15, [5])
        finish(15, 2)
